import numpy as np
import ml_dtypes


def mxq(x, axis, fmt="e4m3"):
    dtype, down = {"e4m3": (ml_dtypes.float8_e4m3fn, 7), "e5m2": (ml_dtypes.float8_e5m2, 14)}[fmt]
    v = np.moveaxis(np.asarray(x, np.float32).astype(ml_dtypes.bfloat16).astype(np.float64), axis, -1)
    blocks = v.reshape(v.shape[:-1] + (-1, 32))
    amax = np.abs(blocks).max(-1, keepdims=True)
    byte = np.maximum(np.where(amax > 0, np.frexp(amax)[1] - 1 + 127, 0) - down, 1)
    scale = np.exp2(byte - 127.0)
    codes = (blocks / scale).astype(np.float32).astype(dtype).astype(np.float64)
    return np.moveaxis((codes * scale).reshape(v.shape), -1, axis)


WIDE = False


def mx_kscale(k):
    if not WIDE:
        return np.ones(k)
    levels = np.array([10, -10, 5, -5, 0])
    if k % 512:
        return np.exp2(np.random.permutation(np.resize(levels, k // 32))).repeat(32)
    a = np.empty((k // 512, 16))
    for p in range(k // 512):
        a[p, :8] = np.random.permutation(np.resize(levels, 8))
        for g in range(8):
            far = levels[np.abs(levels - a[p, g]) >= 10]
            a[p, g + 8] = far[np.random.randint(len(far))]
    return np.exp2(a.ravel()).repeat(32)


def f64(x):
    return np.asarray(x).astype(np.float64)


def striped(idx):
    return np.tile(idx.reshape(-1, 16).T, (8, 1)).astype(np.uint16)


def unstriped(offs):
    return offs[:16].T.reshape(-1).astype(np.int64)


K, T, E, C, N = 1536, 1280, 15, 256, 128
TOP = 3


def by_expert(wq, xq):
    return np.concatenate([wq[e].T @ xq[:, e * C:(e + 1) * C] for e in range(E)], axis=1)


def setup_inputs():
    n = np.random.standard_normal
    s = mx_kscale(K)[:, None]
    deal = np.repeat(np.arange(E), C).reshape(TOP, T)[:, np.random.permutation(T)]
    deal = np.take_along_axis(deal, np.argsort(np.random.rand(TOP, T), axis=0), axis=0)
    for _ in range(8):
        s_, t_ = np.random.permutation(T).reshape(2, -1); r = np.random.randint(TOP, size=T // 2); x, y = deal[r, s_].copy(), deal[r, t_].copy()
        ok = ~((deal[:, s_] == y).any(0) | (deal[:, t_] == x).any(0)); deal[r[ok], s_[ok]] = y[ok]; deal[r[ok], t_[ok]] = x[ok]
    order = np.lexsort((np.random.rand(TOP * T), deal.reshape(-1)))
    slot_token = order % T; pos = np.empty(TOP * T, np.int64); pos[order] = np.arange(TOP * T); pos = pos.reshape(TOP, T)
    g = np.random.uniform(0.5, 1.5, (TOP, T)); g = g / g.sum(0)
    return {
        "xT": (n((K, T)) * s).astype(np.float32),
        "w": (n((E, K, N)) / np.sqrt(K) / s[None]).astype(np.float32),
        "b": (0.3 * n((N, E))).astype(np.float32),
        "gate": np.stack([np.tile(r, (N, 1)) for r in g]).astype(np.float32),
        "offs": striped(slot_token),
        "pos1": striped(pos[0]),
        "pos2": striped(pos[1]),
        "pos3": striped(pos[2]),
    }


def reference(xT, w, b, gate, offs, pos1, pos2, pos3):
    idx = unstriped(offs)
    xq = mxq(f64(xT)[:, idx], 0, "e4m3")
    y = by_expert(mxq(f64(w), 1, "e4m3"), xq)
    y = y + np.repeat(f64(b), C, axis=1)
    return sum(f64(gate[r]) * y[:, unstriped(p)] for r, p in enumerate((pos1, pos2, pos3)))

@@ -1,0 +1,188 @@
+from contextlib import ExitStack
+
+import concourse.mybir as mybir
+
+F32 = mybir.dt.float32
+BF16 = mybir.dt.bfloat16
+U32 = mybir.dt.uint32
+U16 = mybir.dt.uint16
+U8 = mybir.dt.uint8
+FP8X4 = mybir.dt.float8_e4m3fn_x4
+IDENTITY = mybir.ActivationFunctionType.Identity
+MULT = mybir.AluOpType.mult
+ADD = mybir.AluOpType.add
+
+P = 128
+PACK = 4
+PASS_K = P * PACK
+FLOPS = 2 * 1536 * 128 * 3840
+
+TOKEN_CHUNKS = ((0, 512), (512, 512), (1024, 256))
+WEIGHT_UNITS = 4
+GPSIMD_CHUNKS = (4, 6, 8, 10)
+GROUPS = (768, 768, 768, 768, 512, 256)
+OUT_CHUNKS = ((0, 512), (512, 512), (1024, 256))
+
+
+def tile_moe_tk_lin_bias_kernel(tc, xT, w, b, gate, offs, pos1, pos2, pos3, out):
+    nc = tc.nc
+    K, T = xT.shape
+    E, N = w.shape[0], w.shape[2]
+    S = offs.shape[1] * 16
+    C = S // E
+    passes = K // PASS_K
+    units = E * passes
+    x_view = xT.rearrange("(a p j) t -> a p j t", p=P, j=PACK)
+    w_view = w.rearrange("e (a p j) n -> p (e a) (j n)", p=P, j=PACK)
+
+    with ExitStack() as ctx:
+        held = ctx.enter_context(tc.tile_pool(name="held", bufs=1))
+        raws = ctx.enter_context(tc.tile_pool(name="raws", bufs=7))
+        rounds = ctx.enter_context(tc.tile_pool(name="rounds", bufs=11))
+        psum = ctx.enter_context(tc.psum_pool(name="psum", bufs=8))
+
+        offs_sb = held.tile([P, S // 16], U16, name="offs_sb")
+        pos_sb = [held.tile([P, T // 16], U16, name=f"pos{r}_sb") for r in range(3)]
+        gates = held.tile([P, 3, T], F32, name="gates")
+        x_codes = [held.tile([P, T], U32, name=f"x_codes{a}", align_bytes=64) for a in range(passes)]
+        x_scales = held.tile([P, T], U8, name="x_scales", align_bytes=64)
+        s_codes = {}
+        s_scales = {}
+        w_codes = []
+        w_scales = []
+        y = held.tile([P, S], F32, name="y")
+
+        nc.gpsimd.memset(x_scales[:], 0)
+
+        raw_x = {}
+
+        def load_x(a):
+            for t0, tw in TOKEN_CHUNKS:
+                raw = raws.tile([P, PACK, tw], F32, name="raw")
+                nc.sync.dma_start(raw[:], x_view[a][:, :, t0 : t0 + tw])
+                raw_x[a, t0] = raw
+
+        def quantize_x(a, chunk):
+            for t0, tw in (TOKEN_CHUNKS[chunk],):
+                raw = raw_x[a, t0]
+                rounded = rounds.tile([P, tw, PACK], BF16, name="rounded", align_bytes=64)
+                if a == 0:
+                    vec = tw if t0 != 512 else 256
+                else:
+                    vec = 0
+                turned = raw[:].rearrange("p j t -> p t j")
+                if vec:
+                    nc.vector.tensor_copy(rounded[:, :vec, :], turned[:, :vec, :])
+                if vec < tw:
+                    nc.scalar.copy(rounded[:, vec:, :], turned[:, vec:, :])
+                nc.vector.quantize_mx(
+                    out=x_codes[a][:, t0 : t0 + tw].bitcast(FP8X4),
+                    scales=x_scales[4 * a : P, t0 : t0 + tw],
+                    in_=rounded[:].rearrange("p t j -> p (t j)"),
+                )
+
+        raw_w = {}
+
+        def load_w(u0, n_units):
+            raw = raws.tile([P, n_units, PACK * N], F32, name="raw")
+            nc.sync.dma_start(raw[:], w_view[:, u0 : u0 + n_units, :])
+            raw_w[u0] = raw
+
+        def quantize_w(u0, n_units):
+            raw = raw_w[u0]
+            rounded = rounds.tile([P, n_units, N, PACK], BF16, name="rounded", align_bytes=64)
+            codes = held.tile([P, n_units, N], U32, name=f"w_codes{u0}", align_bytes=64)
+            scales = held.tile([P, n_units, N], U8, name=f"w_scales{u0}", align_bytes=64)
+            for i in range(n_units):
+                w_codes.append(codes[:, i, :])
+                w_scales.append(scales[:, i, :])
+            turned = raw[:].rearrange("p u (j n) -> p u n j", j=PACK)
+            if u0 // WEIGHT_UNITS in GPSIMD_CHUNKS:
+                nc.gpsimd.tensor_scalar(rounded[:], turned, 1.0, 0.0, MULT, ADD)
+            else:
+                nc.scalar.copy(rounded[:], turned)
+            nc.vector.quantize_mx(
+                out=codes[:].rearrange("p u n -> p (u n)").bitcast(FP8X4),
+                scales=scales[:].rearrange("p u n -> p (u n)"),
+                in_=rounded[:].rearrange("p u n j -> p (u n j)"),
+            )
+
+        def gather(src, s0, sw, dtype, label):
+            dst = held.tile([P, sw], dtype, name=f"{label}_{s0}", align_bytes=64)
+            nc.vector.tensor_copy(dst[:], src[:].indirect(offs_sb[:, s0 // 16 : (s0 + sw) // 16]))
+            return dst
+
+        chunks = [(u0, min(WEIGHT_UNITS, units - u0)) for u0 in range(0, units, WEIGHT_UNITS)]
+        starts = [sum(GROUPS[:g]) for g in range(len(GROUPS))]
+
+        load_x(0)
+        nc.sync.dma_start(offs_sb[:], offs)
+        load_x(1)
+        for chunk in chunks[:3]:
+            load_w(*chunk)
+        load_x(2)
+        for chunk in chunks[3:]:
+            load_w(*chunk)
+        bias = raws.tile([P, E], F32, tag="raw", name="bias")
+        nc.sync.dma_start(bias[:], b)
+        for tile, pos in zip(pos_sb, (pos1, pos2, pos3)):
+            nc.sync.dma_start(tile[:], pos)
+        nc.sync.dma_start(gates[:], gate.rearrange("r p t -> p r t"))
+
+        for chunk in range(3):
+            quantize_x(0, chunk)
+        made = [0]
+
+        def next_w():
+            if made[0] < len(chunks):
+                quantize_w(*chunks[made[0]])
+                made[0] += 1
+
+        for a in range(passes - 1):
+            for g, (s0, sw) in enumerate(zip(starts, GROUPS)):
+                s_codes[a, g] = gather(x_codes[a], s0, sw, U32, f"s_codes{a}")
+                if a == 0 and g < 3:
+                    quantize_x(1, g)
+                elif a == 1 and g < 3:
+                    next_w()
+        for chunk in range(3):
+            quantize_x(2, chunk)
+
+        accs = {}
+        bank = None
+        for g, (s0, sw) in enumerate(zip(starts, GROUPS)):
+            s_scales[g] = gather(x_scales, s0, sw, U8, "s_scales")
+            next_w()
+            s_codes[passes - 1, g] = gather(x_codes[passes - 1], s0, sw, U32, f"s_codes{passes - 1}")
+            next_w()
+            while len(w_codes) < passes * (s0 + sw) // C:
+                next_w()
+            for e in range(s0 // C, (s0 + sw) // C):
+                cols = slice(e * C - s0, (e + 1) * C - s0)
+                if e % 2 == 0:
+                    bank = psum.tile([P, 2, C], F32, name="bank")
+                acc = bank[:, e % 2, :]
+                for a in range(passes):
+                    nc.tensor.matmul_mx(
+                        out=acc,
+                        lhsT=w_codes[passes * e + a].bitcast(FP8X4),
+                        lhsT_scale=w_scales[passes * e + a],
+                        rhs=s_codes[a, g][:, cols].bitcast(FP8X4),
+                        rhs_scale=s_scales[g][4 * a : P, cols],
+                        start=(a == 0),
+                        stop=(a == passes - 1),
+                    )
+                accs[e] = acc
+        for e in range(E):
+            nc.scalar.activation(y[:, e * C : (e + 1) * C], accs[e], IDENTITY, bias=bias[:, e : e + 1])
+
+        for t0, tw in OUT_CHUNKS:
+            terms = raws.tile([P, 3, tw], F32, tag="raw", name="terms")
+            for r in range(3):
+                nc.vector.tensor_tensor(
+                    terms[:, r, :], y[:].indirect(pos_sb[r][:, t0 // 16 : (t0 + tw) // 16]), gates[:, r, t0 : t0 + tw], MULT
+                )
+            sums = raws.tile([P, 2, tw], F32, tag="raw", name="sums")
+            nc.vector.tensor_tensor(sums[:, 0, :], terms[:, 0, :], terms[:, 1, :], ADD)
+            nc.vector.tensor_tensor(sums[:, 1, :], sums[:, 0, :], terms[:, 2, :], ADD)
+            nc.sync.dma_start(out[:, t0 : t0 + tw], sums[:, 1, :])

@@ -17,9 +17,10 @@ PACK = 4
 PASS_K = P * PACK
 FLOPS = 2 * 1536 * 128 * 3840
 
-TOKEN_CHUNKS = ((0, 512), (512, 512), (1024, 256))
+TOKEN_CHUNKS = ((0, 512, 0), (512, 512, 0), (1024, 256, 0))
 WEIGHT_UNITS = 4
-GPSIMD_CHUNKS = (4, 6, 8, 10)
+X0_CHUNKS = ((0, 512, 512), (512, 512, 256), (1024, 128, 0), (1152, 128, 128))
+EARLY = 960
 GROUPS = (768, 768, 768, 768, 512, 256)
 OUT_CHUNKS = ((0, 512), (512, 512), (1024, 256))
 
@@ -37,7 +38,7 @@ def tile_moe_tk_lin_bias_kernel(tc, xT, w, b, gate, offs, pos1, pos2, pos3, out)
 
     with ExitStack() as ctx:
         held = ctx.enter_context(tc.tile_pool(name="held", bufs=1))
-        raws = ctx.enter_context(tc.tile_pool(name="raws", bufs=7))
+        raws = ctx.enter_context(tc.tile_pool(name="raws", bufs=8))
         rounds = ctx.enter_context(tc.tile_pool(name="rounds", bufs=11))
         psum = ctx.enter_context(tc.psum_pool(name="psum", bufs=8))
 
@@ -46,8 +47,8 @@ def tile_moe_tk_lin_bias_kernel(tc, xT, w, b, gate, offs, pos1, pos2, pos3, out)
         gates = held.tile([P, 3, T], F32, name="gates")
         x_codes = [held.tile([P, T], U32, name=f"x_codes{a}", align_bytes=64) for a in range(passes)]
         x_scales = held.tile([P, T], U8, name="x_scales", align_bytes=64)
-        s_codes = {}
-        s_scales = {}
+        s_codes = [held.tile([P, S], U32, name=f"s_codes{a}", align_bytes=64) for a in range(passes)]
+        s_scales = held.tile([P, S], U8, name="s_scales", align_bytes=64)
         w_codes = []
         w_scales = []
         y = held.tile([P, S], F32, name="y")
@@ -57,24 +58,22 @@ def tile_moe_tk_lin_bias_kernel(tc, xT, w, b, gate, offs, pos1, pos2, pos3, out)
         raw_x = {}
 
         def load_x(a):
-            for t0, tw in TOKEN_CHUNKS:
+            for t0, tw, vec in X0_CHUNKS if a == 0 else TOKEN_CHUNKS:
                 raw = raws.tile([P, PACK, tw], F32, name="raw")
                 nc.sync.dma_start(raw[:], x_view[a][:, :, t0 : t0 + tw])
                 raw_x[a, t0] = raw
 
         def quantize_x(a, chunk):
-            for t0, tw in (TOKEN_CHUNKS[chunk],):
+            for t0, tw, vec in ((X0_CHUNKS if a == 0 else TOKEN_CHUNKS)[chunk],):
                 raw = raw_x[a, t0]
                 rounded = rounds.tile([P, tw, PACK], BF16, name="rounded", align_bytes=64)
-                if a == 0:
-                    vec = tw if t0 != 512 else 256
-                else:
-                    vec = 0
-                turned = raw[:].rearrange("p j t -> p t j")
+                src = raw[:].rearrange("p j (c i) -> p c j i", i=4)
+                dst = rounded[:].rearrange("p (c i) j -> p c j i", i=4)
+                cut = vec // 4
                 if vec:
-                    nc.vector.tensor_copy(rounded[:, :vec, :], turned[:, :vec, :])
+                    nc.vector.tensor_copy(dst[:, :cut], src[:, :cut])
                 if vec < tw:
-                    nc.scalar.copy(rounded[:, vec:, :], turned[:, vec:, :])
+                    nc.scalar.copy(dst[:, cut:], src[:, cut:])
                 nc.vector.quantize_mx(
                     out=x_codes[a][:, t0 : t0 + tw].bitcast(FP8X4),
                     scales=x_scales[4 * a : P, t0 : t0 + tw],
@@ -96,21 +95,17 @@ def tile_moe_tk_lin_bias_kernel(tc, xT, w, b, gate, offs, pos1, pos2, pos3, out)
             for i in range(n_units):
                 w_codes.append(codes[:, i, :])
                 w_scales.append(scales[:, i, :])
-            turned = raw[:].rearrange("p u (j n) -> p u n j", j=PACK)
-            if u0 // WEIGHT_UNITS in GPSIMD_CHUNKS:
-                nc.gpsimd.tensor_scalar(rounded[:], turned, 1.0, 0.0, MULT, ADD)
-            else:
-                nc.scalar.copy(rounded[:], turned)
+            nc.scalar.copy(
+                rounded[:].rearrange("p u (c i) j -> p u c j i", i=4), raw[:].rearrange("p u (j c i) -> p u c j i", j=PACK, i=4)
+            )
             nc.vector.quantize_mx(
                 out=codes[:].rearrange("p u n -> p (u n)").bitcast(FP8X4),
                 scales=scales[:].rearrange("p u n -> p (u n)"),
                 in_=rounded[:].rearrange("p u n j -> p (u n j)"),
             )
 
-        def gather(src, s0, sw, dtype, label):
-            dst = held.tile([P, sw], dtype, name=f"{label}_{s0}", align_bytes=64)
-            nc.vector.tensor_copy(dst[:], src[:].indirect(offs_sb[:, s0 // 16 : (s0 + sw) // 16]))
-            return dst
+        def gather(dst, src, s0, sw):
+            nc.vector.tensor_copy(dst[:, s0 : s0 + sw], src[:].indirect(offs_sb[:, s0 // 16 : (s0 + sw) // 16]))
 
         chunks = [(u0, min(WEIGHT_UNITS, units - u0)) for u0 in range(0, units, WEIGHT_UNITS)]
         starts = [sum(GROUPS[:g]) for g in range(len(GROUPS))]
@@ -121,15 +116,19 @@ def tile_moe_tk_lin_bias_kernel(tc, xT, w, b, gate, offs, pos1, pos2, pos3, out)
         for chunk in chunks[:3]:
             load_w(*chunk)
         load_x(2)
-        for chunk in chunks[3:]:
+        for chunk in chunks[3:9]:
             load_w(*chunk)
-        bias = raws.tile([P, E], F32, tag="raw", name="bias")
-        nc.sync.dma_start(bias[:], b)
+        bias_low = raws.tile([P, 8], F32, tag="raw", name="bias_low")
+        nc.sync.dma_start(bias_low[:], b[:, 0:8])
+        for chunk in chunks[9:]:
+            load_w(*chunk)
+        bias_high = raws.tile([P, E - 8], F32, tag="raw", name="bias_high")
+        nc.sync.dma_start(bias_high[:], b[:, 8:E])
         for tile, pos in zip(pos_sb, (pos1, pos2, pos3)):
             nc.sync.dma_start(tile[:], pos)
         nc.sync.dma_start(gates[:], gate.rearrange("r p t -> p r t"))
 
-        for chunk in range(3):
+        for chunk in range(4):
             quantize_x(0, chunk)
         made = [0]
 
@@ -139,8 +138,8 @@ def tile_moe_tk_lin_bias_kernel(tc, xT, w, b, gate, offs, pos1, pos2, pos3, out)
                 made[0] += 1
 
         for a in range(passes - 1):
-            for g, (s0, sw) in enumerate(zip(starts, GROUPS)):
-                s_codes[a, g] = gather(x_codes[a], s0, sw, U32, f"s_codes{a}")
+            for g in range(S // EARLY):
+                gather(s_codes[a], x_codes[a], g * EARLY, EARLY)
                 if a == 0 and g < 3:
                     quantize_x(1, g)
                 elif a == 1 and g < 3:
@@ -151,14 +150,14 @@ def tile_moe_tk_lin_bias_kernel(tc, xT, w, b, gate, offs, pos1, pos2, pos3, out)
         accs = {}
         bank = None
         for g, (s0, sw) in enumerate(zip(starts, GROUPS)):
-            s_scales[g] = gather(x_scales, s0, sw, U8, "s_scales")
+            gather(s_scales, x_scales, s0, sw)
             next_w()
-            s_codes[passes - 1, g] = gather(x_codes[passes - 1], s0, sw, U32, f"s_codes{passes - 1}")
+            gather(s_codes[passes - 1], x_codes[passes - 1], s0, sw)
             next_w()
             while len(w_codes) < passes * (s0 + sw) // C:
                 next_w()
             for e in range(s0 // C, (s0 + sw) // C):
-                cols = slice(e * C - s0, (e + 1) * C - s0)
+                cols = slice(e * C, (e + 1) * C)
                 if e % 2 == 0:
                     bank = psum.tile([P, 2, C], F32, name="bank")
                 acc = bank[:, e % 2, :]
@@ -167,14 +166,15 @@ def tile_moe_tk_lin_bias_kernel(tc, xT, w, b, gate, offs, pos1, pos2, pos3, out)
                         out=acc,
                         lhsT=w_codes[passes * e + a].bitcast(FP8X4),
                         lhsT_scale=w_scales[passes * e + a],
-                        rhs=s_codes[a, g][:, cols].bitcast(FP8X4),
-                        rhs_scale=s_scales[g][4 * a : P, cols],
+                        rhs=s_codes[a][:, cols].bitcast(FP8X4),
+                        rhs_scale=s_scales[4 * a : P, cols],
                         start=(a == 0),
                         stop=(a == passes - 1),
                     )
                 accs[e] = acc
         for e in range(E):
-            nc.scalar.activation(y[:, e * C : (e + 1) * C], accs[e], IDENTITY, bias=bias[:, e : e + 1])
+            column = bias_low[:, e : e + 1] if e < 8 else bias_high[:, e - 8 : e - 7]
+            nc.scalar.activation(y[:, e * C : (e + 1) * C], accs[e], IDENTITY, bias=column)
 
         for t0, tw in OUT_CHUNKS:
             terms = raws.tile([P, 3, tw], F32, tag="raw", name="terms")

@@ -19,7 +19,7 @@ FLOPS = 2 * 1536 * 128 * 3840
 
 TOKEN_CHUNKS = ((0, 512, 0), (512, 512, 0), (1024, 256, 0))
 WEIGHT_UNITS = 4
-X0_CHUNKS = ((0, 512, 512), (512, 512, 256), (1024, 128, 0), (1152, 128, 128))
+X0_CHUNKS = ((0, 512, 512), (512, 512, 256), (1024, 256, 160))
 EARLY = 960
 GROUPS = (768, 768, 768, 768, 512, 256)
 OUT_CHUNKS = ((0, 512), (512, 512), (1024, 256))
@@ -128,7 +128,7 @@ def tile_moe_tk_lin_bias_kernel(tc, xT, w, b, gate, offs, pos1, pos2, pos3, out)
             nc.sync.dma_start(tile[:], pos)
         nc.sync.dma_start(gates[:], gate.rearrange("r p t -> p r t"))
 
-        for chunk in range(4):
+        for chunk in range(3):
             quantize_x(0, chunk)
         made = [0]
 
@@ -176,13 +176,36 @@ def tile_moe_tk_lin_bias_kernel(tc, xT, w, b, gate, offs, pos1, pos2, pos3, out)
             column = bias_low[:, e : e + 1] if e < 8 else bias_high[:, e - 8 : e - 7]
             nc.scalar.activation(y[:, e * C : (e + 1) * C], accs[e], IDENTITY, bias=column)
 
+        terms = []
+        sums = []
         for t0, tw in OUT_CHUNKS:
-            terms = raws.tile([P, 3, tw], F32, tag="raw", name="terms")
-            for r in range(3):
-                nc.vector.tensor_tensor(
-                    terms[:, r, :], y[:].indirect(pos_sb[r][:, t0 // 16 : (t0 + tw) // 16]), gates[:, r, t0 : t0 + tw], MULT
-                )
-            sums = raws.tile([P, 2, tw], F32, tag="raw", name="sums")
-            nc.vector.tensor_tensor(sums[:, 0, :], terms[:, 0, :], terms[:, 1, :], ADD)
-            nc.vector.tensor_tensor(sums[:, 1, :], sums[:, 0, :], terms[:, 2, :], ADD)
-            nc.sync.dma_start(out[:, t0 : t0 + tw], sums[:, 1, :])
+            terms.append(raws.tile([P, 3, tw], F32, tag="raw", name="terms"))
+            sums.append(raws.tile([P, 2, tw], F32, tag="raw", name="sums"))
+
+        def weigh(i, r):
+            t0, tw = OUT_CHUNKS[i]
+            nc.vector.tensor_tensor(
+                terms[i][:, r, :], y[:].indirect(pos_sb[r][:, t0 // 16 : (t0 + tw) // 16]), gates[:, r, t0 : t0 + tw], MULT
+            )
+
+        def add(i, step):
+            t0, tw = OUT_CHUNKS[i]
+            first = terms[i][:, 0, :] if step == 0 else sums[i][:, 0, :]
+            nc.vector.tensor_tensor(sums[i][:, step, :], first, terms[i][:, step + 1, :], ADD)
+            if step == 1:
+                nc.sync.dma_start(out[:, t0 : t0 + tw], sums[i][:, 1, :])
+
+        for r in range(3):
+            weigh(0, r)
+        weigh(1, 0)
+        add(0, 0)
+        weigh(1, 1)
+        add(0, 1)
+        weigh(1, 2)
+        weigh(2, 0)
+        add(1, 0)
+        weigh(2, 1)
+        weigh(2, 2)
+        add(2, 0)
+        add(1, 1)
+        add(2, 1)

@@ -21,6 +21,7 @@ TOKEN_CHUNKS = ((0, 512, 0), (512, 512, 0), (1024, 256, 0))
 WEIGHT_UNITS = 4
 X0_CHUNKS = ((0, 512, 512), (512, 512, 256), (1024, 256, 160))
 EARLY = 960
+GPSIMD_CHUNKS = (3, 6)
 GROUPS = (768, 768, 768, 768, 512, 256)
 OUT_CHUNKS = ((0, 512), (512, 512), (1024, 256))
 
@@ -95,9 +96,13 @@ def tile_moe_tk_lin_bias_kernel(tc, xT, w, b, gate, offs, pos1, pos2, pos3, out)
             for i in range(n_units):
                 w_codes.append(codes[:, i, :])
                 w_scales.append(scales[:, i, :])
-            nc.scalar.copy(
-                rounded[:].rearrange("p u (c i) j -> p u c j i", i=4), raw[:].rearrange("p u (j c i) -> p u c j i", j=PACK, i=4)
-            )
+            src = raw[:].rearrange("p u (j c i) -> p u c j i", j=PACK, i=4)
+            dst = rounded[:].rearrange("p u (c i) j -> p u c j i", i=4)
+            if u0 // WEIGHT_UNITS in GPSIMD_CHUNKS:
+                for i in range(n_units):
+                    nc.gpsimd.tensor_scalar(dst[:, i], src[:, i], 1.0, 0.0, MULT, ADD)
+            else:
+                nc.scalar.copy(dst, src)
             nc.vector.quantize_mx(
                 out=codes[:].rearrange("p u n -> p (u n)").bitcast(FP8X4),
                 scales=scales[:].rearrange("p u n -> p (u n)"),

@@ -22,6 +22,7 @@ WEIGHT_UNITS = 4
 X0_CHUNKS = ((0, 512, 512), (512, 512, 256), (1024, 256, 160))
 EARLY = 960
 GPSIMD_CHUNKS = (3, 6)
+LATE_AFTER = (4, 5, 7, 8, 10)
 GROUPS = (768, 768, 768, 768, 512, 256)
 OUT_CHUNKS = ((0, 512), (512, 512), (1024, 256))
 
@@ -40,7 +41,7 @@ def tile_moe_tk_lin_bias_kernel(tc, xT, w, b, gate, offs, pos1, pos2, pos3, out)
     with ExitStack() as ctx:
         held = ctx.enter_context(tc.tile_pool(name="held", bufs=1))
         raws = ctx.enter_context(tc.tile_pool(name="raws", bufs=8))
-        rounds = ctx.enter_context(tc.tile_pool(name="rounds", bufs=11))
+        rounds = ctx.enter_context(tc.tile_pool(name="rounds", bufs=7))
         psum = ctx.enter_context(tc.psum_pool(name="psum", bufs=8))
 
         offs_sb = held.tile([P, S // 16], U16, name="offs_sb")
@@ -48,7 +49,7 @@ def tile_moe_tk_lin_bias_kernel(tc, xT, w, b, gate, offs, pos1, pos2, pos3, out)
         gates = held.tile([P, 3, T], F32, name="gates")
         x_codes = [held.tile([P, T], U32, name=f"x_codes{a}", align_bytes=64) for a in range(passes)]
         x_scales = held.tile([P, T], U8, name="x_scales", align_bytes=64)
-        s_codes = [held.tile([P, S], U32, name=f"s_codes{a}", align_bytes=64) for a in range(passes)]
+        s_codes = [held.tile([P, S], U32, name=f"s_codes{a}", align_bytes=64) for a in range(passes - 1)]
         s_scales = held.tile([P, S], U8, name="s_scales", align_bytes=64)
         w_codes = []
         w_scales = []
@@ -58,8 +59,8 @@ def tile_moe_tk_lin_bias_kernel(tc, xT, w, b, gate, offs, pos1, pos2, pos3, out)
 
         raw_x = {}
 
-        def load_x(a):
-            for t0, tw, vec in X0_CHUNKS if a == 0 else TOKEN_CHUNKS:
+        def load_x(a, token_chunks):
+            for t0, tw, vec in token_chunks:
                 raw = raws.tile([P, PACK, tw], F32, name="raw")
                 nc.sync.dma_start(raw[:], x_view[a][:, :, t0 : t0 + tw])
                 raw_x[a, t0] = raw
@@ -90,7 +91,11 @@ def tile_moe_tk_lin_bias_kernel(tc, xT, w, b, gate, offs, pos1, pos2, pos3, out)
 
         def quantize_w(u0, n_units):
             raw = raw_w[u0]
-            rounded = rounds.tile([P, n_units, N, PACK], BF16, name="rounded", align_bytes=64)
+            chunk = u0 // WEIGHT_UNITS
+            if chunk in LATE_AFTER:
+                rounded = held.tile([P, n_units, N, PACK], BF16, tag=f"late{chunk}", name="rounded_late", align_bytes=64)
+            else:
+                rounded = rounds.tile([P, n_units, N, PACK], BF16, name="rounded", align_bytes=64)
             codes = held.tile([P, n_units, N], U32, name=f"w_codes{u0}", align_bytes=64)
             scales = held.tile([P, n_units, N], U8, name=f"w_scales{u0}", align_bytes=64)
             for i in range(n_units):
@@ -115,13 +120,14 @@ def tile_moe_tk_lin_bias_kernel(tc, xT, w, b, gate, offs, pos1, pos2, pos3, out)
         chunks = [(u0, min(WEIGHT_UNITS, units - u0)) for u0 in range(0, units, WEIGHT_UNITS)]
         starts = [sum(GROUPS[:g]) for g in range(len(GROUPS))]
 
-        load_x(0)
+        load_x(0, X0_CHUNKS[:1])
         nc.sync.dma_start(offs_sb[:], offs)
-        load_x(1)
-        for chunk in chunks[:3]:
+        load_x(0, X0_CHUNKS[1:])
+        load_x(1, TOKEN_CHUNKS)
+        for chunk in chunks[:2]:
             load_w(*chunk)
-        load_x(2)
-        for chunk in chunks[3:9]:
+        load_x(2, TOKEN_CHUNKS)
+        for chunk in chunks[2:9]:
             load_w(*chunk)
         bias_low = raws.tile([P, 8], F32, tag="raw", name="bias_low")
         nc.sync.dma_start(bias_low[:], b[:, 0:8])
@@ -147,7 +153,7 @@ def tile_moe_tk_lin_bias_kernel(tc, xT, w, b, gate, offs, pos1, pos2, pos3, out)
                 gather(s_codes[a], x_codes[a], g * EARLY, EARLY)
                 if a == 0 and g < 3:
                     quantize_x(1, g)
-                elif a == 1 and g < 3:
+                elif a == 1 and g < 2:
                     next_w()
         for chunk in range(3):
             quantize_x(2, chunk)
@@ -155,9 +161,13 @@ def tile_moe_tk_lin_bias_kernel(tc, xT, w, b, gate, offs, pos1, pos2, pos3, out)
         accs = {}
         bank = None
         for g, (s0, sw) in enumerate(zip(starts, GROUPS)):
-            gather(s_scales, x_scales, s0, sw)
-            next_w()
-            gather(s_codes[passes - 1], x_codes[passes - 1], s0, sw)
+            if g < S // EARLY:
+                gather(s_scales, x_scales, g * EARLY, EARLY)
+            while made[0] <= (LATE_AFTER[g - 1] if g else 2):
+                next_w()
+            tag = f"late{LATE_AFTER[g - 1]}" if g else "early"
+            late = held.tile([P, sw], U32, tag=tag, name="late_codes", align_bytes=64)
+            nc.vector.tensor_copy(late[:], x_codes[passes - 1][:].indirect(offs_sb[:, s0 // 16 : (s0 + sw) // 16]))
             next_w()
             while len(w_codes) < passes * (s0 + sw) // C:
                 next_w()
@@ -166,12 +176,13 @@ def tile_moe_tk_lin_bias_kernel(tc, xT, w, b, gate, offs, pos1, pos2, pos3, out)
                 if e % 2 == 0:
                     bank = psum.tile([P, 2, C], F32, name="bank")
                 acc = bank[:, e % 2, :]
+                words = [codes[:, cols] for codes in s_codes] + [late[:, e * C - s0 : (e + 1) * C - s0]]
                 for a in range(passes):
                     nc.tensor.matmul_mx(
                         out=acc,
                         lhsT=w_codes[passes * e + a].bitcast(FP8X4),
                         lhsT_scale=w_scales[passes * e + a],
-                        rhs=s_codes[a][:, cols].bitcast(FP8X4),
+                        rhs=words[a].bitcast(FP8X4),
                         rhs_scale=s_scales[4 * a : P, cols],
                         start=(a == 0),
                         stop=(a == passes - 1),

from contextlib import ExitStack

import concourse.mybir as mybir

F32 = mybir.dt.float32
BF16 = mybir.dt.bfloat16
U32 = mybir.dt.uint32
U16 = mybir.dt.uint16
U8 = mybir.dt.uint8
FP8X4 = mybir.dt.float8_e4m3fn_x4
IDENTITY = mybir.ActivationFunctionType.Identity
MULT = mybir.AluOpType.mult
ADD = mybir.AluOpType.add

P = 128
PACK = 4
PASS_K = P * PACK
FLOPS = 2 * 1536 * 128 * 3840

TOKEN_CHUNKS = ((0, 512, 0), (512, 512, 0), (1024, 256, 0))
WEIGHT_UNITS = 4
X0_CHUNKS = ((0, 512, 512), (512, 512, 256), (1024, 256, 160))
EARLY = 960
GPSIMD_CHUNKS = (3, 6)
LATE_AFTER = (4, 5, 7, 8, 10)
GROUPS = (768, 768, 768, 768, 512, 256)
OUT_CHUNKS = ((0, 512), (512, 512), (1024, 256))


def tile_moe_tk_lin_bias_kernel(tc, xT, w, b, gate, offs, pos1, pos2, pos3, out):
    nc = tc.nc
    K, T = xT.shape
    E, N = w.shape[0], w.shape[2]
    S = offs.shape[1] * 16
    C = S // E
    passes = K // PASS_K
    units = E * passes
    x_view = xT.rearrange("(a p j) t -> a p j t", p=P, j=PACK)
    w_view = w.rearrange("e (a p j) n -> p (e a) (j n)", p=P, j=PACK)

    with ExitStack() as ctx:
        held = ctx.enter_context(tc.tile_pool(name="held", bufs=1))
        raws = ctx.enter_context(tc.tile_pool(name="raws", bufs=8))
        rounds = ctx.enter_context(tc.tile_pool(name="rounds", bufs=7))
        psum = ctx.enter_context(tc.psum_pool(name="psum", bufs=8))

        offs_sb = held.tile([P, S // 16], U16, name="offs_sb")
        pos_sb = [held.tile([P, T // 16], U16, name=f"pos{r}_sb") for r in range(3)]
        gates = held.tile([P, 3, T], F32, name="gates")
        x_codes = [held.tile([P, T], U32, name=f"x_codes{a}", align_bytes=64) for a in range(passes)]
        x_scales = held.tile([P, T], U8, name="x_scales", align_bytes=64)
        s_codes = [held.tile([P, S], U32, name=f"s_codes{a}", align_bytes=64) for a in range(passes - 1)]
        s_scales = held.tile([P, S], U8, name="s_scales", align_bytes=64)
        w_codes = []
        w_scales = []
        y = held.tile([P, S], F32, name="y")

        nc.gpsimd.memset(x_scales[:], 0)

        raw_x = {}

        def load_x(a, token_chunks):
            for t0, tw, vec in token_chunks:
                raw = raws.tile([P, PACK, tw], F32, name="raw")
                nc.sync.dma_start(raw[:], x_view[a][:, :, t0 : t0 + tw])
                raw_x[a, t0] = raw

        def quantize_x(a, chunk):
            for t0, tw, vec in ((X0_CHUNKS if a == 0 else TOKEN_CHUNKS)[chunk],):
                raw = raw_x[a, t0]
                rounded = rounds.tile([P, tw, PACK], BF16, name="rounded", align_bytes=64)
                src = raw[:].rearrange("p j (c i) -> p c j i", i=4)
                dst = rounded[:].rearrange("p (c i) j -> p c j i", i=4)
                cut = vec // 4
                if vec:
                    nc.vector.tensor_copy(dst[:, :cut], src[:, :cut])
                if vec < tw:
                    nc.scalar.copy(dst[:, cut:], src[:, cut:])
                nc.vector.quantize_mx(
                    out=x_codes[a][:, t0 : t0 + tw].bitcast(FP8X4),
                    scales=x_scales[4 * a : P, t0 : t0 + tw],
                    in_=rounded[:].rearrange("p t j -> p (t j)"),
                )

        raw_w = {}

        def load_w(u0, n_units):
            raw = raws.tile([P, n_units, PACK * N], F32, name="raw")
            nc.sync.dma_start(raw[:], w_view[:, u0 : u0 + n_units, :])
            raw_w[u0] = raw

        def quantize_w(u0, n_units):
            raw = raw_w[u0]
            chunk = u0 // WEIGHT_UNITS
            if chunk in LATE_AFTER:
                rounded = held.tile([P, n_units, N, PACK], BF16, tag=f"late{chunk}", name="rounded_late", align_bytes=64)
            else:
                rounded = rounds.tile([P, n_units, N, PACK], BF16, name="rounded", align_bytes=64)
            codes = held.tile([P, n_units, N], U32, name=f"w_codes{u0}", align_bytes=64)
            scales = held.tile([P, n_units, N], U8, name=f"w_scales{u0}", align_bytes=64)
            for i in range(n_units):
                w_codes.append(codes[:, i, :])
                w_scales.append(scales[:, i, :])
            src = raw[:].rearrange("p u (j c i) -> p u c j i", j=PACK, i=4)
            dst = rounded[:].rearrange("p u (c i) j -> p u c j i", i=4)
            if u0 // WEIGHT_UNITS in GPSIMD_CHUNKS:
                for i in range(n_units):
                    nc.gpsimd.tensor_scalar(dst[:, i], src[:, i], 1.0, 0.0, MULT, ADD)
            else:
                nc.scalar.copy(dst, src)
            nc.vector.quantize_mx(
                out=codes[:].rearrange("p u n -> p (u n)").bitcast(FP8X4),
                scales=scales[:].rearrange("p u n -> p (u n)"),
                in_=rounded[:].rearrange("p u n j -> p (u n j)"),
            )

        def gather(dst, src, s0, sw):
            nc.vector.tensor_copy(dst[:, s0 : s0 + sw], src[:].indirect(offs_sb[:, s0 // 16 : (s0 + sw) // 16]))

        chunks = [(u0, min(WEIGHT_UNITS, units - u0)) for u0 in range(0, units, WEIGHT_UNITS)]
        starts = [sum(GROUPS[:g]) for g in range(len(GROUPS))]

        load_x(0, X0_CHUNKS[:1])
        nc.sync.dma_start(offs_sb[:], offs)
        load_x(0, X0_CHUNKS[1:])
        load_x(1, TOKEN_CHUNKS)
        for chunk in chunks[:2]:
            load_w(*chunk)
        load_x(2, TOKEN_CHUNKS)
        for chunk in chunks[2:9]:
            load_w(*chunk)
        bias_low = raws.tile([P, 8], F32, tag="raw", name="bias_low")
        nc.sync.dma_start(bias_low[:], b[:, 0:8])
        for chunk in chunks[9:]:
            load_w(*chunk)
        bias_high = raws.tile([P, E - 8], F32, tag="raw", name="bias_high")
        nc.sync.dma_start(bias_high[:], b[:, 8:E])
        for tile, pos in zip(pos_sb, (pos1, pos2, pos3)):
            nc.sync.dma_start(tile[:], pos)
        nc.sync.dma_start(gates[:], gate.rearrange("r p t -> p r t"))

        for chunk in range(3):
            quantize_x(0, chunk)
        made = [0]

        def next_w():
            if made[0] < len(chunks):
                quantize_w(*chunks[made[0]])
                made[0] += 1

        for a in range(passes - 1):
            for g in range(S // EARLY):
                gather(s_codes[a], x_codes[a], g * EARLY, EARLY)
                if a == 0 and g < 3:
                    quantize_x(1, g)
                elif a == 1 and g < 2:
                    next_w()
        for chunk in range(3):
            quantize_x(2, chunk)

        accs = {}
        bank = None
        for g, (s0, sw) in enumerate(zip(starts, GROUPS)):
            if g < S // EARLY:
                gather(s_scales, x_scales, g * EARLY, EARLY)
            while made[0] <= (LATE_AFTER[g - 1] if g else 2):
                next_w()
            tag = f"late{LATE_AFTER[g - 1]}" if g else "early"
            late = held.tile([P, sw], U32, tag=tag, name="late_codes", align_bytes=64)
            nc.vector.tensor_copy(late[:], x_codes[passes - 1][:].indirect(offs_sb[:, s0 // 16 : (s0 + sw) // 16]))
            next_w()
            while len(w_codes) < passes * (s0 + sw) // C:
                next_w()
            for e in range(s0 // C, (s0 + sw) // C):
                cols = slice(e * C, (e + 1) * C)
                if e % 2 == 0:
                    bank = psum.tile([P, 2, C], F32, name="bank")
                acc = bank[:, e % 2, :]
                words = [codes[:, cols] for codes in s_codes] + [late[:, e * C - s0 : (e + 1) * C - s0]]
                for a in range(passes):
                    nc.tensor.matmul_mx(
                        out=acc,
                        lhsT=w_codes[passes * e + a].bitcast(FP8X4),
                        lhsT_scale=w_scales[passes * e + a],
                        rhs=words[a].bitcast(FP8X4),
                        rhs_scale=s_scales[4 * a : P, cols],
                        start=(a == 0),
                        stop=(a == passes - 1),
                    )
                accs[e] = acc
        for e in range(E):
            column = bias_low[:, e : e + 1] if e < 8 else bias_high[:, e - 8 : e - 7]
            nc.scalar.activation(y[:, e * C : (e + 1) * C], accs[e], IDENTITY, bias=column)

        terms = []
        sums = []
        for t0, tw in OUT_CHUNKS:
            terms.append(raws.tile([P, 3, tw], F32, tag="raw", name="terms"))
            sums.append(raws.tile([P, 2, tw], F32, tag="raw", name="sums"))

        def weigh(i, r):
            t0, tw = OUT_CHUNKS[i]
            nc.vector.tensor_tensor(
                terms[i][:, r, :], y[:].indirect(pos_sb[r][:, t0 // 16 : (t0 + tw) // 16]), gates[:, r, t0 : t0 + tw], MULT
            )

        def add(i, step):
            t0, tw = OUT_CHUNKS[i]
            first = terms[i][:, 0, :] if step == 0 else sums[i][:, 0, :]
            nc.vector.tensor_tensor(sums[i][:, step, :], first, terms[i][:, step + 1, :], ADD)
            if step == 1:
                nc.sync.dma_start(out[:, t0 : t0 + tw], sums[i][:, 1, :])

        for r in range(3):
            weigh(0, r)
        weigh(1, 0)
        add(0, 0)
        weigh(1, 1)
        add(0, 1)
        weigh(1, 2)
        weigh(2, 0)
        add(1, 0)
        weigh(2, 1)
        weigh(2, 2)
        add(2, 0)
        add(1, 1)
        add(2, 1)
